import numpy as np
import ml_dtypes


def mxq(x, axis, fmt="e4m3"):
    dtype, down = {"e4m3": (ml_dtypes.float8_e4m3fn, 7), "e5m2": (ml_dtypes.float8_e5m2, 14)}[fmt]
    v = np.moveaxis(np.asarray(x, np.float32).astype(ml_dtypes.bfloat16).astype(np.float64), axis, -1)
    blocks = v.reshape(v.shape[:-1] + (-1, 32))
    amax = np.abs(blocks).max(-1, keepdims=True)
    byte = np.maximum(np.where(amax > 0, np.frexp(amax)[1] - 1 + 127, 0) - down, 1)
    scale = np.exp2(byte - 127.0)
    codes = (blocks / scale).astype(np.float32).astype(dtype).astype(np.float64)
    return np.moveaxis((codes * scale).reshape(v.shape), -1, axis)


WIDE = False


def mx_kscale(k):
    if not WIDE:
        return np.ones(k)
    levels = np.array([10, -10, 5, -5, 0])
    if k % 512:
        return np.exp2(np.random.permutation(np.resize(levels, k // 32))).repeat(32)
    a = np.empty((k // 512, 16))
    for p in range(k // 512):
        a[p, :8] = np.random.permutation(np.resize(levels, 8))
        for g in range(8):
            far = levels[np.abs(levels - a[p, g]) >= 10]
            a[p, g + 8] = far[np.random.randint(len(far))]
    return np.exp2(a.ravel()).repeat(32)


def f64(x):
    return np.asarray(x).astype(np.float64)


def striped(idx):
    return np.tile(np.asarray(idx).reshape(-1, 16).T, (8, 1)).astype(np.uint16)


def unstriped(offs):
    return offs[:16].T.reshape(-1).astype(np.int64)


E2M1 = np.array([0.0, 0.5, 1.0, 1.5, 2.0, 3.0, 4.0, 6.0, -0.0, -0.5, -1.0, -1.5, -2.0, -3.0, -4.0, -6.0])


def pack_weight(w, fmt):
    k, n = w.shape
    w = f64(np.asarray(w, np.float32).astype(ml_dtypes.bfloat16)).reshape(k // 32, 32, n)
    amax = np.abs(w).max(1)
    if fmt == "e4m3":
        byte = np.frexp(amax)[1] - 1 + 127 - 7
    else:
        mant, ex = np.frexp(amax / 6.0)
        byte = np.where(mant > 0.5, ex, ex - 1) + 127
    byte = np.clip(np.where(amax > 0, byte, 1), 1, 254)
    scaled = (w * np.exp2(127.0 - byte)[:, None, :]).reshape(k, n).astype(np.float32)
    by_word = np.ascontiguousarray(scaled.reshape(k // 512, 128, 4, n).transpose(0, 1, 3, 2))
    if fmt == "e4m3":
        words = by_word.astype(ml_dtypes.float8_e4m3fn).view(np.uint8)
    else:
        c = by_word.astype(ml_dtypes.float4_e2m1fn).view(np.uint8) & 0xF
        words = (c[..., 0::2] | (c[..., 1::2] << 4)).reshape(k // 512, 128, 2 * n)
    return np.ascontiguousarray(words), np.ascontiguousarray(byte.astype(np.uint8).reshape(k // 512, 16, n))


def unpack_weight(words, scales, fmt):
    g, _, n = scales.shape
    words = np.ascontiguousarray(words).reshape(g, 128, n, -1)
    if fmt == "e4m3":
        vals = words.view(ml_dtypes.float8_e4m3fn).astype(np.float64)
    else:
        nib = np.empty((g, 128, n, 4), np.uint8)
        nib[..., 0::2] = words & 0xF
        nib[..., 1::2] = words >> 4
        vals = E2M1[nib]
    vals = vals * np.repeat(np.exp2(scales.astype(np.float64) - 127.0), 8, axis=1)[..., None]
    return vals.transpose(0, 1, 3, 2).reshape(g * 512, n)


K, L, T, C, V, J = 1024, 512, 256, 2048, 1024, 512


def setup_inputs():
    n = np.random.standard_normal
    idx = np.random.permutation(C)[:J]
    idx2 = np.random.permutation(V)[:J]
    fk = mx_kscale(K)
    fl = mx_kscale(L)
    wcp = pack_weight(n((K, C)) * 1 / np.sqrt(K) * fk[:, None], "e4m3")
    xlp = pack_weight(n((L, T)) * 0.5 / fl[:, None], "e2m1")
    wlp = pack_weight(n((L, V)) * 1 / np.sqrt(L) * fl[:, None], "e4m3")
    return {
        "xt": (n((K, T)) * 0.5 / fk[:, None]).astype(np.float32),
        "wc_words": wcp[0],
        "wc_scales": wcp[1],
        "xl_words": xlp[0],
        "xl_scales": xlp[1],
        "wl_words": wlp[0],
        "wl_scales": wlp[1],
        "offs": striped(idx),
        "offs2": striped(idx2),
    }


def reference(xt, wc_words, wc_scales, xl_words, xl_scales, wl_words, wl_scales, offs, offs2):
    idx = unstriped(offs)
    idx2 = unstriped(offs2)
    wcu = unpack_weight(wc_words, wc_scales, "e4m3")
    xlu = unpack_weight(xl_words, xl_scales, "e2m1")
    wlu = unpack_weight(wl_words, wl_scales, "e4m3")
    xtq = mxq(f64(xt), 0, "e4m3")
    wcidxg = wcu[:, idx]
    za = xtq.T @ wcidxg
    wlidx2g = wlu[:, idx2]
    zb = xlu.T @ wlidx2g
    p = np.exp(za + zb)
    y = 512.0 * p / np.sum(p, axis=1, keepdims=True)
    return y

@@ -1,0 +1,123 @@
+from contextlib import ExitStack
+
+import concourse.mybir as mybir
+
+K, L, T, C, V, J = 1024, 512, 256, 2048, 1024, 512
+FLOPS = 2 * T * J * (K + L)
+
+F32 = mybir.dt.float32
+BF16 = mybir.dt.bfloat16
+I32 = mybir.dt.int32
+U32 = mybir.dt.uint32
+U16 = mybir.dt.uint16
+U8 = mybir.dt.uint8
+FP8X4 = mybir.dt.float8_e4m3fn_x4
+FP4X4 = mybir.dt.float4_e2m1fn_x4
+ALU = mybir.AluOpType
+ACT = mybir.ActivationFunctionType
+
+P = 128
+PACK = 4
+K_PASS = P * PACK
+HALF = J // 2
+
+
+def tile_list_joint_scores_of_two_models_kernel(
+    tc, xt, wc_words, wc_scales, xl_words, xl_scales, wl_words, wl_scales, offs, offs2, out
+):
+    nc = tc.nc
+    with ExitStack() as ctx:
+        sb = ctx.enter_context(tc.tile_pool(name="sb", bufs=1))
+        ps = ctx.enter_context(tc.psum_pool(name="ps", bufs=1))
+
+        def tile(name, shape, dtype):
+            return sb.tile(shape, dtype, name=name, align_bytes=64)
+
+        idx_c = tile("idx_c", [P, J // 16], U16)
+        idx_l = tile("idx_l", [P, J // 16], U16)
+        wcs = tile("wcs", [P, C], U8)
+        wls = tile("wls", [P, V], U8)
+        xls = tile("xls", [P, T], U8)
+        xlw = tile("xlw", [P, 2 * T], U8)
+        wlw = tile("wlw", [P, V], U32)
+        wcw = [tile("wcw%d" % a, [P, C], U32) for a in range(2)]
+        raw = [tile("raw%d" % a, [P, PACK, T], F32) for a in range(2)]
+
+        nc.vector.memset(wcs[:].bitcast(I32), 0)
+        nc.vector.memset(wls[:].bitcast(I32), 0)
+        nc.vector.memset(xls[:].bitcast(I32), 0)
+
+        for q in range(4):
+            nc.scalar.dma_start(wcs[32 * q : 32 * q + 8, :].bitcast(I32), wc_scales[:, 4 * q : 4 * q + 4, :].bitcast(I32))
+        for q in range(4):
+            nc.scalar.dma_start(wls[32 * q : 32 * q + 4, :].bitcast(I32), wl_scales[:, 4 * q : 4 * q + 4, :].bitcast(I32))
+        for q in range(4):
+            nc.gpsimd.dma_start(xls[32 * q : 32 * q + 4, :].bitcast(I32), xl_scales[:, 4 * q : 4 * q + 4, :].bitcast(I32))
+        nc.sync.dma_start(raw[0][:], xt[0 * K_PASS : 1 * K_PASS, :].rearrange("(p j) t -> p j t", j=PACK))
+        nc.sync.dma_start(idx_c[:], offs)
+        nc.sync.dma_start(raw[1][:], xt[1 * K_PASS : 2 * K_PASS, :].rearrange("(p j) t -> p j t", j=PACK))
+        nc.sync.dma_start(idx_l[:], offs2)
+        nc.sync.dma_start(wlw[:].bitcast(I32), wl_words[0].rearrange("p n t -> p (n t)").bitcast(I32))
+        nc.sync.dma_start(xlw[:].bitcast(I32), xl_words[0].bitcast(I32))
+        nc.sync.dma_start(wcw[0][:].bitcast(I32), wc_words[0].rearrange("p n t -> p (n t)").bitcast(I32))
+        nc.sync.dma_start(wcw[1][:].bitcast(I32), wc_words[1].rearrange("p n t -> p (n t)").bitcast(I32))
+
+
+        xq = [tile("xq%d" % a, [P, T], U32) for a in range(2)]
+        xqs = [tile("xqs%d" % a, [P, T], U8) for a in range(2)]
+        for a in range(2):
+            grouped = tile("grouped%d" % a, [P, T, PACK], BF16)
+            nc.scalar.copy(
+                grouped[:].rearrange("p (c i) j -> p c j i", i=4),
+                raw[a][:].rearrange("p j (c i) -> p c j i", i=4),
+            )
+            nc.vector.quantize_mx(
+                out=xq[a][:].bitcast(FP8X4), scales=xqs[a][:], in_=grouped[:].rearrange("p t j -> p (t j)")
+            )
+
+        g_lw = tile("g_lw", [P, J], U32)
+        g_ls = tile("g_ls", [P, J], U8)
+        g_cs = tile("g_cs", [P, J], U8)
+        g_c0 = tile("g_c0", [P, J], U32)
+        g_c1 = [tile("g_c1_%d" % h, [P, HALF], U32) for h in range(2)]
+        nc.vector.tensor_copy(g_cs[:], wcs[:].indirect(idx_c[:]))
+        nc.vector.tensor_copy(g_lw[:], wlw[:].indirect(idx_l[:]))
+        nc.vector.tensor_copy(g_ls[:], wls[:].indirect(idx_l[:]))
+        nc.vector.tensor_copy(g_c0[:], wcw[0][:].indirect(idx_c[:]))
+        for h in range(2):
+            nc.vector.tensor_copy(g_c1[h][:], wcw[1][:].indirect(idx_c[:, 16 * h : 16 * (h + 1)]))
+
+        z = [ps.tile([P, J], F32, name="z%d" % m) for m in range(2)]
+        for m in range(2):
+            tok = slice(m * P, (m + 1) * P)
+            nc.tensor.matmul_mx(
+                out=z[m][:], lhsT=xq[0][:, tok].bitcast(FP8X4), lhsT_scale=xqs[0][:, tok],
+                rhs=g_c0[:].bitcast(FP8X4), rhs_scale=g_cs[:], start=True, stop=False,
+            )
+        for m in range(2):
+            tok = slice(m * P, (m + 1) * P)
+            nc.tensor.matmul_mx(
+                out=z[m][:], lhsT=xlw[:, 2 * m * P : 2 * (m + 1) * P].bitcast(FP4X4), lhsT_scale=xls[:, tok],
+                rhs=g_lw[:].bitcast(FP8X4), rhs_scale=g_ls[:], start=False, stop=False,
+            )
+        for h in range(2):
+            cols = slice(h * HALF, (h + 1) * HALF)
+            for m in range(2):
+                tok = slice(m * P, (m + 1) * P)
+                nc.tensor.matmul_mx(
+                    out=z[m][:, cols], lhsT=xq[1][:, tok].bitcast(FP8X4), lhsT_scale=xqs[1][:, tok],
+                    rhs=g_c1[h][:].bitcast(FP8X4), rhs_scale=g_cs[4:, cols], start=False, stop=(h == 1),
+                )
+
+        neg_max = [tile("neg_max%d" % m, [P, 1], F32) for m in range(2)]
+        for m in range(2):
+            nc.vector.reduce_max(neg_max[m][:], z[m][:], mybir.AxisListType.X, negate=True)
+        for m in range(2):
+            e = tile("e%d" % m, [P, J], F32)
+            total = tile("total%d" % m, [P, 1], F32)
+            inv = tile("inv%d" % m, [P, 1], F32)
+            y = tile("y%d" % m, [P, J], F32)
+            nc.scalar.activation(e[:], z[m][:], ACT.Exp, bias=neg_max[m][:], scale=1.0, accum_out=total[:])
+            nc.vector.reciprocal(inv[:], total[:])
+            nc.vector.tensor_scalar(y[:], e[:], inv[:], float(J), ALU.mult, ALU.mult)
+            nc.sync.dma_start(out[m * P : (m + 1) * P, :], y[:])

@@ -30,13 +30,13 @@ def tile_list_joint_scores_of_two_models_kernel(
         sb = ctx.enter_context(tc.tile_pool(name="sb", bufs=1))
         ps = ctx.enter_context(tc.psum_pool(name="ps", bufs=1))
 
-        def tile(name, shape, dtype):
-            return sb.tile(shape, dtype, name=name, align_bytes=64)
+        def tile(name, shape, dtype, tag=None):
+            return sb.tile(shape, dtype, name=name, tag=tag or name, align_bytes=64)
 
         idx_c = tile("idx_c", [P, J // 16], U16)
         idx_l = tile("idx_l", [P, J // 16], U16)
         wcs = tile("wcs", [P, C], U8)
-        wls = tile("wls", [P, V], U8)
+        wls = tile("wls", [P, V], U8, tag="wls_then_xqs1")
         xls = tile("xls", [P, T], U8)
         xlw = tile("xlw", [P, 2 * T], U8)
         wlw = tile("wlw", [P, V], U32)
@@ -45,34 +45,38 @@ def tile_list_joint_scores_of_two_models_kernel(
 
         nc.vector.memset(wcs[:].bitcast(I32), 0)
         nc.vector.memset(wls[:].bitcast(I32), 0)
-        nc.vector.memset(xls[:].bitcast(I32), 0)
 
-        for q in range(4):
-            nc.scalar.dma_start(wcs[32 * q : 32 * q + 8, :].bitcast(I32), wc_scales[:, 4 * q : 4 * q + 4, :].bitcast(I32))
-        for q in range(4):
-            nc.scalar.dma_start(wls[32 * q : 32 * q + 4, :].bitcast(I32), wl_scales[:, 4 * q : 4 * q + 4, :].bitcast(I32))
-        for q in range(4):
-            nc.gpsimd.dma_start(xls[32 * q : 32 * q + 4, :].bitcast(I32), xl_scales[:, 4 * q : 4 * q + 4, :].bitcast(I32))
-        nc.sync.dma_start(raw[0][:], xt[0 * K_PASS : 1 * K_PASS, :].rearrange("(p j) t -> p j t", j=PACK))
-        nc.sync.dma_start(idx_c[:], offs)
-        nc.sync.dma_start(raw[1][:], xt[1 * K_PASS : 2 * K_PASS, :].rearrange("(p j) t -> p j t", j=PACK))
-        nc.sync.dma_start(idx_l[:], offs2)
         nc.sync.dma_start(wlw[:].bitcast(I32), wl_words[0].rearrange("p n t -> p (n t)").bitcast(I32))
-        nc.sync.dma_start(xlw[:].bitcast(I32), xl_words[0].bitcast(I32))
+        nc.sync.dma_start(idx_l[:], offs2)
+        nc.sync.dma_start(idx_c[:], offs)
+        for q in range(4):
+            nc.sync.dma_start(
+                xls[32 * q : 32 * q + 32, :].bitcast(I32),
+                xl_scales[:, 4 * q : 4 * q + 4, :].bitcast(I32).to_broadcast([8, 4, T // 4]),
+            )
         nc.sync.dma_start(wcw[0][:].bitcast(I32), wc_words[0].rearrange("p n t -> p (n t)").bitcast(I32))
+        for q in range(4):
+            nc.sync.dma_start(wcs[32 * q : 32 * q + 8, :].bitcast(I32), wc_scales[:, 4 * q : 4 * q + 4, :].bitcast(I32))
+        nc.sync.dma_start(raw[0][:], xt[0 * K_PASS : 1 * K_PASS, :].rearrange("(p j) t -> p j t", j=PACK))
+        nc.sync.dma_start(raw[1][:], xt[1 * K_PASS : 2 * K_PASS, :].rearrange("(p j) t -> p j t", j=PACK))
+        nc.sync.dma_start(xlw[:].bitcast(I32), xl_words[0].bitcast(I32))
+        for q in range(4):
+            nc.sync.dma_start(wls[32 * q : 32 * q + 4, :].bitcast(I32), wl_scales[:, 4 * q : 4 * q + 4, :].bitcast(I32))
         nc.sync.dma_start(wcw[1][:].bitcast(I32), wc_words[1].rearrange("p n t -> p (n t)").bitcast(I32))
 
 
-        xq = [tile("xq%d" % a, [P, T], U32) for a in range(2)]
-        xqs = [tile("xqs%d" % a, [P, T], U8) for a in range(2)]
+        grouped = [tile("grouped%d" % a, [P, T, PACK], BF16) for a in range(2)]
         for a in range(2):
-            grouped = tile("grouped%d" % a, [P, T, PACK], BF16)
             nc.scalar.copy(
-                grouped[:].rearrange("p (c i) j -> p c j i", i=4),
+                grouped[a][:].rearrange("p (c i) j -> p c j i", i=4),
                 raw[a][:].rearrange("p j (c i) -> p c j i", i=4),
             )
+        xq = [tile("xq%d" % a, [P, T], U32) for a in range(2)]
+        xqs = [tile("xqs0", [P, T], U8)]
+
+        def quantize(a):
             nc.vector.quantize_mx(
-                out=xq[a][:].bitcast(FP8X4), scales=xqs[a][:], in_=grouped[:].rearrange("p t j -> p (t j)")
+                out=xq[a][:].bitcast(FP8X4), scales=xqs[a][:], in_=grouped[a][:].rearrange("p t j -> p (t j)")
             )
 
         g_lw = tile("g_lw", [P, J], U32)
@@ -80,44 +84,60 @@ def tile_list_joint_scores_of_two_models_kernel(
         g_cs = tile("g_cs", [P, J], U8)
         g_c0 = tile("g_c0", [P, J], U32)
         g_c1 = [tile("g_c1_%d" % h, [P, HALF], U32) for h in range(2)]
-        nc.vector.tensor_copy(g_cs[:], wcs[:].indirect(idx_c[:]))
         nc.vector.tensor_copy(g_lw[:], wlw[:].indirect(idx_l[:]))
-        nc.vector.tensor_copy(g_ls[:], wls[:].indirect(idx_l[:]))
         nc.vector.tensor_copy(g_c0[:], wcw[0][:].indirect(idx_c[:]))
+        nc.vector.tensor_copy(g_cs[:], wcs[:].indirect(idx_c[:]))
+        quantize(0)
+        nc.vector.tensor_copy(g_ls[:], wls[:].indirect(idx_l[:]))
+        xqs.append(tile("xqs1", [P, T], U8, tag="wls_then_xqs1"))
+        quantize(1)
         for h in range(2):
             nc.vector.tensor_copy(g_c1[h][:], wcw[1][:].indirect(idx_c[:, 16 * h : 16 * (h + 1)]))
 
-        z = [ps.tile([P, J], F32, name="z%d" % m) for m in range(2)]
+        z = [[ps.tile([P, HALF], F32, name="z%d_%d" % (m, h)) for h in range(2)] for m in range(2)]
         for m in range(2):
             tok = slice(m * P, (m + 1) * P)
-            nc.tensor.matmul_mx(
-                out=z[m][:], lhsT=xq[0][:, tok].bitcast(FP8X4), lhsT_scale=xqs[0][:, tok],
-                rhs=g_c0[:].bitcast(FP8X4), rhs_scale=g_cs[:], start=True, stop=False,
-            )
+            for h in range(2):
+                cols = slice(h * HALF, (h + 1) * HALF)
+                nc.tensor.matmul_mx(
+                    out=z[m][h][:], lhsT=xq[0][:, tok].bitcast(FP8X4), lhsT_scale=xqs[0][:, tok],
+                    rhs=g_c0[:, cols].bitcast(FP8X4), rhs_scale=g_cs[:, cols], start=True, stop=False,
+                )
         for m in range(2):
             tok = slice(m * P, (m + 1) * P)
-            nc.tensor.matmul_mx(
-                out=z[m][:], lhsT=xlw[:, 2 * m * P : 2 * (m + 1) * P].bitcast(FP4X4), lhsT_scale=xls[:, tok],
-                rhs=g_lw[:].bitcast(FP8X4), rhs_scale=g_ls[:], start=False, stop=False,
-            )
+            for c in range(4):
+                cols = slice(c * P, (c + 1) * P)
+                nc.tensor.matmul_mx(
+                    out=z[m][c // 2][:, (c % 2) * P : (c % 2 + 1) * P],
+                    lhsT=xlw[:, 2 * m * P : 2 * (m + 1) * P].bitcast(FP4X4), lhsT_scale=xls[:, tok],
+                    rhs=g_lw[:, cols].bitcast(FP8X4), rhs_scale=g_ls[:, cols], start=False, stop=False,
+                )
         for h in range(2):
             cols = slice(h * HALF, (h + 1) * HALF)
             for m in range(2):
                 tok = slice(m * P, (m + 1) * P)
                 nc.tensor.matmul_mx(
-                    out=z[m][:, cols], lhsT=xq[1][:, tok].bitcast(FP8X4), lhsT_scale=xqs[1][:, tok],
-                    rhs=g_c1[h][:].bitcast(FP8X4), rhs_scale=g_cs[4:, cols], start=False, stop=(h == 1),
+                    out=z[m][h][:], lhsT=xq[1][:, tok].bitcast(FP8X4), lhsT_scale=xqs[1][:, tok],
+                    rhs=g_c1[h][:].bitcast(FP8X4), rhs_scale=g_cs[4:, cols], start=False, stop=True,
                 )
 
-        neg_max = [tile("neg_max%d" % m, [P, 1], F32) for m in range(2)]
+        neg_z = [tile("neg_z%d" % m, [P, J], F32) for m in range(2)]
+        neg_max = [[tile("neg_max%d_%d" % (m, h), [P, 1], F32) for h in range(2)] for m in range(2)]
         for m in range(2):
-            nc.vector.reduce_max(neg_max[m][:], z[m][:], mybir.AxisListType.X, negate=True)
+            for h in range(2):
+                cols = slice(h * HALF, (h + 1) * HALF)
+                nc.vector.tensor_scalar(
+                    neg_z[m][:, cols], z[m][h][:], -1.0, neg_max[m][0][:] if h else None,
+                    ALU.mult, ALU.min, accum_out=neg_max[m][h][:],
+                )
         for m in range(2):
             e = tile("e%d" % m, [P, J], F32)
             total = tile("total%d" % m, [P, 1], F32)
             inv = tile("inv%d" % m, [P, 1], F32)
-            y = tile("y%d" % m, [P, J], F32)
-            nc.scalar.activation(e[:], z[m][:], ACT.Exp, bias=neg_max[m][:], scale=1.0, accum_out=total[:])
+            nc.scalar.activation(e[:], neg_z[m][:], ACT.Exp, bias=neg_max[m][1][:], scale=-1.0, accum_out=total[:])
             nc.vector.reciprocal(inv[:], total[:])
-            nc.vector.tensor_scalar(y[:], e[:], inv[:], float(J), ALU.mult, ALU.mult)
-            nc.sync.dma_start(out[m * P : (m + 1) * P, :], y[:])
+            for h in range(2):
+                cols = slice(h * HALF, (h + 1) * HALF)
+                y = tile("y%d_%d" % (m, h), [P, HALF], F32)
+                nc.vector.tensor_scalar(y[:], e[:, cols], inv[:], float(J), ALU.mult, ALU.mult)
+                nc.sync.dma_start(out[m * P : (m + 1) * P, cols], y[:])

from contextlib import ExitStack

import concourse.mybir as mybir

K, L, T, C, V, J = 1024, 512, 256, 2048, 1024, 512
FLOPS = 2 * T * J * (K + L)

F32 = mybir.dt.float32
BF16 = mybir.dt.bfloat16
I32 = mybir.dt.int32
U32 = mybir.dt.uint32
U16 = mybir.dt.uint16
U8 = mybir.dt.uint8
FP8X4 = mybir.dt.float8_e4m3fn_x4
FP4X4 = mybir.dt.float4_e2m1fn_x4
ALU = mybir.AluOpType
ACT = mybir.ActivationFunctionType

P = 128
PACK = 4
K_PASS = P * PACK
HALF = J // 2


def tile_list_joint_scores_of_two_models_kernel(
    tc, xt, wc_words, wc_scales, xl_words, xl_scales, wl_words, wl_scales, offs, offs2, out
):
    nc = tc.nc
    with ExitStack() as ctx:
        sb = ctx.enter_context(tc.tile_pool(name="sb", bufs=1))
        ps = ctx.enter_context(tc.psum_pool(name="ps", bufs=1))

        def tile(name, shape, dtype, tag=None):
            return sb.tile(shape, dtype, name=name, tag=tag or name, align_bytes=64)

        idx_c = tile("idx_c", [P, J // 16], U16)
        idx_l = tile("idx_l", [P, J // 16], U16)
        wcs = tile("wcs", [P, C], U8)
        wls = tile("wls", [P, V], U8, tag="wls_then_xqs1")
        xls = tile("xls", [P, T], U8)
        xlw = tile("xlw", [P, 2 * T], U8)
        wlw = tile("wlw", [P, V], U32)
        wcw = [tile("wcw%d" % a, [P, C], U32) for a in range(2)]
        raw = [tile("raw%d" % a, [P, PACK, T], F32) for a in range(2)]

        nc.vector.memset(wcs[:].bitcast(I32), 0)
        nc.vector.memset(wls[:].bitcast(I32), 0)

        nc.sync.dma_start(wlw[:].bitcast(I32), wl_words[0].rearrange("p n t -> p (n t)").bitcast(I32))
        nc.sync.dma_start(idx_l[:], offs2)
        nc.sync.dma_start(idx_c[:], offs)
        for q in range(4):
            nc.sync.dma_start(
                xls[32 * q : 32 * q + 32, :].bitcast(I32),
                xl_scales[:, 4 * q : 4 * q + 4, :].bitcast(I32).to_broadcast([8, 4, T // 4]),
            )
        nc.sync.dma_start(wcw[0][:].bitcast(I32), wc_words[0].rearrange("p n t -> p (n t)").bitcast(I32))
        for q in range(4):
            nc.sync.dma_start(wcs[32 * q : 32 * q + 8, :].bitcast(I32), wc_scales[:, 4 * q : 4 * q + 4, :].bitcast(I32))
        nc.sync.dma_start(raw[0][:], xt[0 * K_PASS : 1 * K_PASS, :].rearrange("(p j) t -> p j t", j=PACK))
        nc.sync.dma_start(raw[1][:], xt[1 * K_PASS : 2 * K_PASS, :].rearrange("(p j) t -> p j t", j=PACK))
        nc.sync.dma_start(xlw[:].bitcast(I32), xl_words[0].bitcast(I32))
        for q in range(4):
            nc.sync.dma_start(wls[32 * q : 32 * q + 4, :].bitcast(I32), wl_scales[:, 4 * q : 4 * q + 4, :].bitcast(I32))
        nc.sync.dma_start(wcw[1][:].bitcast(I32), wc_words[1].rearrange("p n t -> p (n t)").bitcast(I32))


        grouped = [tile("grouped%d" % a, [P, T, PACK], BF16) for a in range(2)]
        for a in range(2):
            nc.scalar.copy(
                grouped[a][:].rearrange("p (c i) j -> p c j i", i=4),
                raw[a][:].rearrange("p j (c i) -> p c j i", i=4),
            )
        xq = [tile("xq%d" % a, [P, T], U32) for a in range(2)]
        xqs = [tile("xqs0", [P, T], U8)]

        def quantize(a):
            nc.vector.quantize_mx(
                out=xq[a][:].bitcast(FP8X4), scales=xqs[a][:], in_=grouped[a][:].rearrange("p t j -> p (t j)")
            )

        g_lw = tile("g_lw", [P, J], U32)
        g_ls = tile("g_ls", [P, J], U8)
        g_cs = tile("g_cs", [P, J], U8)
        g_c0 = tile("g_c0", [P, J], U32)
        g_c1 = [tile("g_c1_%d" % h, [P, HALF], U32) for h in range(2)]
        nc.vector.tensor_copy(g_lw[:], wlw[:].indirect(idx_l[:]))
        nc.vector.tensor_copy(g_c0[:], wcw[0][:].indirect(idx_c[:]))
        nc.vector.tensor_copy(g_cs[:], wcs[:].indirect(idx_c[:]))
        quantize(0)
        nc.vector.tensor_copy(g_ls[:], wls[:].indirect(idx_l[:]))
        xqs.append(tile("xqs1", [P, T], U8, tag="wls_then_xqs1"))
        quantize(1)
        for h in range(2):
            nc.vector.tensor_copy(g_c1[h][:], wcw[1][:].indirect(idx_c[:, 16 * h : 16 * (h + 1)]))

        z = [[ps.tile([P, HALF], F32, name="z%d_%d" % (m, h)) for h in range(2)] for m in range(2)]
        for m in range(2):
            tok = slice(m * P, (m + 1) * P)
            for h in range(2):
                cols = slice(h * HALF, (h + 1) * HALF)
                nc.tensor.matmul_mx(
                    out=z[m][h][:], lhsT=xq[0][:, tok].bitcast(FP8X4), lhsT_scale=xqs[0][:, tok],
                    rhs=g_c0[:, cols].bitcast(FP8X4), rhs_scale=g_cs[:, cols], start=True, stop=False,
                )
        for m in range(2):
            tok = slice(m * P, (m + 1) * P)
            for c in range(4):
                cols = slice(c * P, (c + 1) * P)
                nc.tensor.matmul_mx(
                    out=z[m][c // 2][:, (c % 2) * P : (c % 2 + 1) * P],
                    lhsT=xlw[:, 2 * m * P : 2 * (m + 1) * P].bitcast(FP4X4), lhsT_scale=xls[:, tok],
                    rhs=g_lw[:, cols].bitcast(FP8X4), rhs_scale=g_ls[:, cols], start=False, stop=False,
                )
        for h in range(2):
            cols = slice(h * HALF, (h + 1) * HALF)
            for m in range(2):
                tok = slice(m * P, (m + 1) * P)
                nc.tensor.matmul_mx(
                    out=z[m][h][:], lhsT=xq[1][:, tok].bitcast(FP8X4), lhsT_scale=xqs[1][:, tok],
                    rhs=g_c1[h][:].bitcast(FP8X4), rhs_scale=g_cs[4:, cols], start=False, stop=True,
                )

        neg_z = [tile("neg_z%d" % m, [P, J], F32) for m in range(2)]
        neg_max = [[tile("neg_max%d_%d" % (m, h), [P, 1], F32) for h in range(2)] for m in range(2)]
        for m in range(2):
            for h in range(2):
                cols = slice(h * HALF, (h + 1) * HALF)
                nc.vector.tensor_scalar(
                    neg_z[m][:, cols], z[m][h][:], -1.0, neg_max[m][0][:] if h else None,
                    ALU.mult, ALU.min, accum_out=neg_max[m][h][:],
                )
        for m in range(2):
            e = tile("e%d" % m, [P, J], F32)
            total = tile("total%d" % m, [P, 1], F32)
            inv = tile("inv%d" % m, [P, 1], F32)
            nc.scalar.activation(e[:], neg_z[m][:], ACT.Exp, bias=neg_max[m][1][:], scale=-1.0, accum_out=total[:])
            nc.vector.reciprocal(inv[:], total[:])
            for h in range(2):
                cols = slice(h * HALF, (h + 1) * HALF)
                y = tile("y%d_%d" % (m, h), [P, HALF], F32)
                nc.vector.tensor_scalar(y[:], e[:, cols], inv[:], float(J), ALU.mult, ALU.mult)
                nc.sync.dma_start(out[m * P : (m + 1) * P, cols], y[:])
